import numpy as np
import ml_dtypes


def mxq(x, axis, fmt="e4m3"):
    dtype, down = {"e4m3": (ml_dtypes.float8_e4m3fn, 7), "e5m2": (ml_dtypes.float8_e5m2, 14)}[fmt]
    v = np.moveaxis(np.asarray(x, np.float32).astype(ml_dtypes.bfloat16).astype(np.float64), axis, -1)
    blocks = v.reshape(v.shape[:-1] + (-1, 32))
    amax = np.abs(blocks).max(-1, keepdims=True)
    byte = np.maximum(np.where(amax > 0, np.frexp(amax)[1] - 1 + 127, 0) - down, 1)
    scale = np.exp2(byte - 127.0)
    codes = (blocks / scale).astype(np.float32).astype(dtype).astype(np.float64)
    return np.moveaxis((codes * scale).reshape(v.shape), -1, axis)


WIDE = False


def mx_kscale(k):
    if not WIDE:
        return np.ones(k)
    levels = np.array([10, -10, 5, -5, 0])
    if k % 512:
        return np.exp2(np.random.permutation(np.resize(levels, k // 32))).repeat(32)
    a = np.empty((k // 512, 16))
    for p in range(k // 512):
        a[p, :8] = np.random.permutation(np.resize(levels, 8))
        for g in range(8):
            far = levels[np.abs(levels - a[p, g]) >= 10]
            a[p, g + 8] = far[np.random.randint(len(far))]
    return np.exp2(a.ravel()).repeat(32)


def f64(x):
    return np.asarray(x).astype(np.float64)


def striped(idx):
    return np.tile(idx.reshape(-1, 16).T, (8, 1)).astype(np.uint16)


def unstriped(offs):
    return offs[:16].T.reshape(-1).astype(np.int64)


E2M1 = np.array([0.0, 0.5, 1.0, 1.5, 2.0, 3.0, 4.0, 6.0, -0.0, -0.5, -1.0, -1.5, -2.0, -3.0, -4.0, -6.0])


def pack_weight(w, fmt):
    k, n = w.shape
    w = f64(np.asarray(w, np.float32).astype(ml_dtypes.bfloat16)).reshape(k // 32, 32, n)
    amax = np.abs(w).max(1)
    if fmt == "e4m3":
        byte = np.frexp(amax)[1] - 1 + 127 - 7
    else:
        mant, ex = np.frexp(amax / 6.0)
        byte = np.where(mant > 0.5, ex, ex - 1) + 127
    byte = np.clip(np.where(amax > 0, byte, 1), 1, 254)
    scaled = (w * np.exp2(127.0 - byte)[:, None, :]).reshape(k, n).astype(np.float32)
    by_word = np.ascontiguousarray(scaled.reshape(k // 512, 128, 4, n).transpose(0, 1, 3, 2))
    if fmt == "e4m3":
        words = by_word.astype(ml_dtypes.float8_e4m3fn).view(np.uint8)
    else:
        c = by_word.astype(ml_dtypes.float4_e2m1fn).view(np.uint8) & 0xF
        words = (c[..., 0::2] | (c[..., 1::2] << 4)).reshape(k // 512, 128, 2 * n)
    return np.ascontiguousarray(words), np.ascontiguousarray(byte.astype(np.uint8).reshape(k // 512, 16, n))


def unpack_weight(words, scales, fmt):
    g, _, n = scales.shape
    words = np.ascontiguousarray(words).reshape(g, 128, n, -1)
    if fmt == "e4m3":
        vals = words.view(ml_dtypes.float8_e4m3fn).astype(np.float64)
    else:
        nib = np.empty((g, 128, n, 4), np.uint8)
        nib[..., 0::2] = words & 0xF
        nib[..., 1::2] = words >> 4
        vals = E2M1[nib]
    vals = vals * np.repeat(np.exp2(scales.astype(np.float64) - 127.0), 8, axis=1)[..., None]
    return vals.transpose(0, 1, 3, 2).reshape(g * 512, n)


def gelu(v):
    return 0.5 * v * (1.0 + np.tanh(np.sqrt(2.0 / np.pi) * (v + 0.044715 * v**3)))


def striped8(idx):
    return np.concatenate([v.reshape(-1, 16).T for v in idx]).astype(np.uint16)


def unstriped8(offs):
    return np.stack([offs[16 * g:16 * g + 16].T.reshape(-1) for g in range(8)]).astype(np.int64)


def heads(h, wgt, idx8):
    r = np.arange(h.shape[0])
    return wgt[r // 4 % 128] * h[r[:, None], idx8[r % 512 // 64]]


K, H, N, T, S, P = 512, 1024, 384, 4096, 1024, 512

def setup_inputs():
    n = np.random.standard_normal
    s = mx_kscale(K)[:, None]
    u = mx_kscale(H)[:, None]
    tab_words, tab_scales = pack_weight(n((K, T)) * s, "e4m3")
    w1 = (n((K, H)) / np.sqrt(K) / s * u.T).astype(np.float32)
    w2_words, w2_scales = pack_weight(n((K, H)) / np.sqrt(K) / s, "e2m1")
    w3 = (n((K, H)) / np.sqrt(K) / s).astype(np.float32)
    w4_words, w4_scales = pack_weight(n((H, N)) / np.sqrt(H) / u, "e2m1")
    wga = np.repeat(np.random.uniform(0.5, 2.0, (8, P)), 16, axis=0).astype(np.float32)
    wgb = np.repeat(np.random.uniform(0.5, 2.0, (8, P)), 16, axis=0).astype(np.float32)
    offs = striped(np.random.permutation(T)[:S])
    offs2 = striped8(np.stack([np.random.permutation(S)[:P] for _ in range(8)]))
    offs3 = striped8(np.stack([np.random.permutation(S)[:P] for _ in range(8)]))
    return {"tab_words": tab_words, "tab_scales": tab_scales, "w1": w1,
            "w2_words": w2_words, "w2_scales": w2_scales, "w3": w3,
            "w4_words": w4_words, "w4_scales": w4_scales,
            "wga": wga, "wgb": wgb, "offs": offs, "offs2": offs2, "offs3": offs3}

def reference(tab_words, tab_scales, w1, w2_words, w2_scales, w3, w4_words, w4_scales, wga, wgb, offs, offs2, offs3):
    v = unpack_weight(tab_words, tab_scales, "e4m3")[:, unstriped(offs)]
    w2 = unpack_weight(w2_words, w2_scales, "e2m1")
    w4 = unpack_weight(w4_words, w4_scales, "e2m1")
    a = mxq(f64(w1), 0, "e4m3").T @ v
    b = w2.T @ v
    c = mxq(f64(w3), 0, "e4m3").T @ v
    h = a * np.maximum(b, c)
    xa = heads(h, f64(wga), unstriped8(offs2))
    xb = heads(h, f64(wgb), unstriped8(offs3))
    d = np.abs(xa - xb)
    y = w4.T @ mxq(d, 0, "e4m3")
    return np.log(1.0 + np.square(y))

@@ -1,0 +1,273 @@
+from contextlib import ExitStack
+
+import concourse.mybir as mybir
+
+K, H, N, T, S, M = 512, 1024, 384, 4096, 1024, 512
+FLOPS = 3 * 2 * K * H * S + 2 * H * N * M
+
+F32 = mybir.dt.float32
+BF16 = mybir.dt.bfloat16
+I32 = mybir.dt.int32
+U32 = mybir.dt.uint32
+U16 = mybir.dt.uint16
+U8 = mybir.dt.uint8
+FP8X4 = mybir.dt.float8_e4m3fn_x4
+FP4X4 = mybir.dt.float4_e2m1fn_x4
+ALU = mybir.AluOpType
+ACT = mybir.ActivationFunctionType
+
+P = 128
+PACK = 4
+PASS = P * PACK
+BANK = 512
+HALVES = S // BANK
+BLOCKS = H // PASS
+SLICES = BLOCKS * PACK
+N_TILES = N // P
+CHUNK = 256
+LATE = 128
+EARLY = M - LATE
+
+
+def tile_list_octopus_pattern_change_kernel(
+    tc, tab_words, tab_scales, w1, w2_words, w2_scales, w3, w4_words, w4_scales, wga, wgb, offs, offs2, offs3, out
+):
+    nc = tc.nc
+    with ExitStack() as ctx:
+        keep = ctx.enter_context(tc.tile_pool(name="keep", bufs=1))
+        ring = ctx.enter_context(tc.tile_pool(name="ring", bufs=2))
+        psum = ctx.enter_context(tc.psum_pool(name="psum", bufs=1))
+
+        def held(shape, dtype, name):
+            return keep.tile(shape, dtype, name=name, align_bytes=64)
+
+        def load_scale_rows(queue, plane, rows):
+            for r in range(4):
+                queue.dma_start(out=plane[r:P:32], in_=rows[r:16:4])
+
+        def held_after(earlier, shape, dtype, name):
+            return keep.tile(shape, dtype, name=name, tag=earlier, align_bytes=64)
+
+        def weight_rows(w, c0, width):
+            return w[:, c0 : c0 + width].rearrange("(p j) c -> p j c", j=PACK)
+
+        list1 = keep.tile([P, S // 16], U16, name="list1")
+        list2 = keep.tile([P, M // 16], U16, name="list2")
+        list3 = keep.tile([P, M // 16], U16, name="list3")
+        nc.sync.dma_start(list1[:], offs)
+
+        table_scales = held([P, T], U8, "table_scales")
+        nc.vector.memset(table_scales[:].bitcast(I32), 0)
+        load_scale_rows(nc.scalar, table_scales[:].bitcast(I32), tab_scales[0].bitcast(I32))
+        w2_plane = held([P, H], U8, "w2_plane")
+        nc.gpsimd.memset(w2_plane[:].bitcast(I32), 0)
+        load_scale_rows(nc.gpsimd, w2_plane[:].bitcast(I32), w2_scales[0].bitcast(I32))
+
+        w2_raw = held([P, 2 * H], U8, "w2_raw")
+        nc.sync.dma_start(out=w2_raw[:].bitcast(I32), in_=w2_words[0].bitcast(I32))
+        raw3_0 = held([P, PACK, PASS], F32, "raw3_0")
+        nc.sync.dma_start(out=raw3_0[:], in_=weight_rows(w3, 0, PASS))
+        nc.sync.dma_start(list2[:], offs2)
+        nc.sync.dma_start(list3[:], offs3)
+        table = held([P, T], U32, "table")
+        nc.sync.dma_start(out=table[:].bitcast(I32), in_=tab_words[0].rearrange("p t i -> p (t i)").bitcast(I32))
+
+        def cast_weight(cast, grouped, raw, c0):
+            width = raw.shape[2]
+            dealt = grouped[:].rearrange("p (i q j) -> p q j i", i=PACK, j=PACK)
+            cast(dealt[:, c0 // PACK : (c0 + width) // PACK], raw[:].rearrange("p j (q i) -> p q j i", i=PACK))
+
+        def on_scalar(dst, src):
+            nc.scalar.activation(out=dst, in_=src, func=ACT.Copy)
+
+        def on_vector(dst, src):
+            nc.vector.tensor_copy(out=dst, in_=src)
+
+        def quantise(grouped, width, name):
+            codes = held([P, width], U32, name + "_codes")
+            scales = held([P, width], U8, name + "_scales")
+            nc.vector.quantize_mx(out=codes[:].bitcast(FP8X4), scales=scales[:], in_=grouped)
+            return codes, scales
+
+        w2_codes = held([P, 2 * H], U8, "w2_codes")
+        w2_dealt = held([P, H], U8, "w2_dealt")
+        for b in range(BLOCKS):
+            pairs = slice(2 * b * PASS, 2 * (b + 1) * PASS)
+            nc.vector.tensor_copy(
+                out=w2_codes[:, pairs].rearrange("p (i q e) -> p q i e", i=PACK, e=2),
+                in_=w2_raw[:, pairs].rearrange("p (q i e) -> p q i e", i=PACK, e=2),
+            )
+        v_scales = held([P, S], U8, "v_scales")
+        nc.vector.tensor_copy(v_scales[:], table_scales[:].indirect(list1[:]))
+        nc.vector.tensor_copy(
+            out=w2_dealt[:].rearrange("p (b i q) -> p b q i", b=BLOCKS, i=PACK),
+            in_=w2_plane[:].rearrange("p (b q i) -> p b q i", b=BLOCKS, i=PACK),
+        )
+
+        grouped3_0 = held([P, PACK * PASS], BF16, "grouped3_0")
+        cast_weight(on_scalar, grouped3_0, raw3_0, 0)
+        mx3 = [quantise(grouped3_0[:], PASS, "w3_0")]
+
+        raw1_0a = held_after("w2_raw", [P, PACK, CHUNK], F32, "raw1_0a")
+        nc.sync.dma_start(out=raw1_0a[:], in_=weight_rows(w1, 0, CHUNK))
+        raw1_0b = held_after("w2_plane", [P, PACK, CHUNK], F32, "raw1_0b")
+        nc.sync.dma_start(out=raw1_0b[:], in_=weight_rows(w1, CHUNK, CHUNK))
+        gains = held_after("raw3_0", [P, 2, M], F32, "gains")
+        gain_a, gain_b = gains[:, 0, :], gains[:, 1, :]
+        nc.sync.dma_start(out=gain_a, in_=wga)
+        nc.sync.dma_start(out=gain_b, in_=wgb)
+
+        v_words = []
+        for hf in range(HALVES):
+            words = held([P, BANK], U32, "v_words_%d" % hf)
+            nc.vector.tensor_copy(words[:], table[:].indirect(list1[:, hf * BANK // 16 : (hf + 1) * BANK // 16]))
+            v_words.append(words)
+        grouped1_0 = held([P, PACK * PASS], BF16, "grouped1_0")
+        cast_weight(on_scalar, grouped1_0, raw1_0a, 0)
+        cast_weight(on_vector, grouped1_0, raw1_0b, CHUNK)
+        mx1 = [quantise(grouped1_0[:], PASS, "w1_0")]
+
+        raw3_1 = held_after("table", [P, PACK, PASS], F32, "raw3_1")
+        nc.sync.dma_start(out=raw3_1[:], in_=weight_rows(w3, PASS, PASS))
+        raw1_1 = held_after("w2_raw", [P, PACK, PASS], F32, "raw1_1")
+        nc.sync.dma_start(out=raw1_1[:], in_=weight_rows(w1, PASS, PASS))
+        w4_codes = held_after("w2_plane", [P, BLOCKS, 2 * N], U8, "w4_codes")
+        nc.sync.dma_start(out=w4_codes[:].bitcast(I32), in_=w4_words.bitcast(I32).rearrange("b p n -> p b n"))
+        w4_plane = held_after("grouped1_0", [P, BLOCKS, N], U8, "w4_plane")
+        nc.gpsimd.memset(w4_plane[:].bitcast(I32), 0)
+        load_scale_rows(nc.sync, w4_plane[:].bitcast(I32), w4_scales.bitcast(I32).rearrange("b q n -> q b n"))
+
+        def second_block(raw, name):
+            grouped = held([P, PACK * PASS], BF16, "grouped" + name)
+            cast_weight(on_scalar, grouped, raw, 0)
+            return quantise(grouped[:], PASS, name)
+
+        def product(tag, bufs, codes, scales, hf):
+            bank = psum.tile([P, BANK], F32, name=tag, tag=tag, bufs=bufs)
+            nc.tensor.matmul_mx(
+                out=bank[:],
+                lhsT=codes,
+                lhsT_scale=scales,
+                rhs=v_words[hf][:].bitcast(FP8X4),
+                rhs_scale=v_scales[:, hf * BANK : (hf + 1) * BANK],
+                start=True,
+                stop=True,
+            )
+            return bank
+
+        def larger(s, hf):
+            b, i = divmod(s, PACK)
+            cols = slice(i * P, (i + 1) * P)
+            bank_b = product(
+                "bank_b", 2, w2_codes[:, 2 * s * P : 2 * (s + 1) * P].bitcast(FP4X4), w2_dealt[:, s * P : (s + 1) * P], hf
+            )
+            bank_c = product("bank_c", 2, mx3[b][0][:, cols].bitcast(FP8X4), mx3[b][1][:, cols], hf)
+            b_sb = ring.tile([P, BANK], F32, name="b_sb", bufs=3)
+            nc.scalar.activation(out=b_sb[:], in_=bank_b[:], func=ACT.Copy)
+            most = ring.tile([P, BANK], F32, name="most", bufs=4)
+            nc.vector.tensor_tensor(out=most[:], in0=bank_c[:], in1=b_sb[:], op=ALU.max)
+            return most
+
+        def feature(s, hf, most, h):
+            b, i = divmod(s, PACK)
+            cols = slice(i * P, (i + 1) * P)
+            bank_a = product("bank_a", 3, mx1[b][0][:, cols].bitcast(FP8X4), mx1[b][1][:, cols], hf)
+            nc.vector.tensor_tensor(out=h[:, hf * BANK : (hf + 1) * BANK], in0=bank_a[:], in1=most[:], op=ALU.mult)
+
+        def pick(h, m0, width, xa=None):
+            picked = []
+            for name, offsets, gain in (("xa", list2, gain_a), ("xb", list3, gain_b)):
+                x = xa if xa is not None and name == "xa" else ring.tile([P, width], F32, name=name, tag=name)
+                nc.vector.tensor_tensor(
+                    out=x[:],
+                    in0=h[:].indirect(offsets[:, m0 // 16 : (m0 + width) // 16]),
+                    in1=gain[:, m0 : m0 + width],
+                    op=ALU.mult,
+                )
+                picked.append(x)
+            return picked
+
+        def round_change(diff, grouped):
+            nc.scalar.activation(
+                out=grouped[:].rearrange("p (c u i) -> p c i u", i=PACK, u=4),
+                in_=diff[:].rearrange("p i (c u) -> p c i u", u=4),
+                func=ACT.Abs,
+            )
+            return grouped
+
+        def score(bank_of, mx_d, ranges, m0, width):
+            for n in range(N_TILES):
+                bank = bank_of(n)
+                for lo, hi in ranges:
+                    for b in range(BLOCKS):
+                        codes, scales, first = mx_d[b]
+                        nc.tensor.matmul_mx(
+                            out=bank[:, lo - m0 : hi - m0],
+                            lhsT=w4_codes[:, b, 2 * n * P : 2 * (n + 1) * P].bitcast(FP4X4),
+                            lhsT_scale=w4_plane[:, b, n * P : (n + 1) * P],
+                            rhs=codes[:, lo - first : hi - first].bitcast(FP8X4),
+                            rhs_scale=scales[:, lo - first : hi - first],
+                            start=(b == 0),
+                            stop=(b == BLOCKS - 1),
+                        )
+
+        def finish(y, width, dst, name):
+            squared = held(list(y.shape), F32, name + "_squared")
+            nc.scalar.activation(out=squared[:], in_=y, func=ACT.Square)
+            result = held(list(y.shape), F32, name + "_result")
+            nc.scalar.activation(out=result[:], in_=squared[:], func=ACT.Ln, bias=1.0)
+            nc.sync.dma_start(out=dst, in_=result[:])
+
+        h = [held([P, S], F32, "h_%d" % s) for s in range(SLICES)]
+        widths = [M, EARLY]
+        diff = [held([P, PACK, widths[b]], F32, "diff_%d" % b) for b in range(BLOCKS)]
+        mx_d = []
+        grouped_d = []
+
+        most = {(0, 0): larger(0, 0)}
+        for s in range(SLICES):
+            b, i = divmod(s, PACK)
+            most[s, 1] = larger(s, 1)
+            feature(s, 0, most[s, 0], h[s])
+            feature(s, 1, most[s, 1], h[s])
+            if s == 1:
+                mx3.append(second_block(raw3_1, "w3_1"))
+            if s == 2:
+                mx1.append(second_block(raw1_1, "w1_1"))
+            if s == PACK + 1:
+                mx_d.append(quantise(grouped_d[0][:], M, "d_0") + (0,))
+            if s + 1 < SLICES:
+                most[s + 1, 0] = larger(s + 1, 0)
+            xa, xb = pick(h[s], 0, widths[b])
+            (nc.gpsimd if s + 1 < SLICES else nc.vector).tensor_tensor(out=diff[b][:, i, :], in0=xa[:], in1=xb[:], op=ALU.subtract)
+            if i == PACK - 1:
+                grouped_d.append(round_change(diff[b], held([P, PACK * widths[b]], BF16, "d_%d_grouped" % b)))
+
+        diff_late = held([P, PACK, LATE], F32, "diff_late")
+
+        def subtract_late(i, xa, xb):
+            nc.vector.tensor_tensor(out=diff_late[:, i, :], in0=xa[:], in1=xb[:], op=ALU.subtract)
+
+        picked = [pick(h[PACK], EARLY, LATE), pick(h[PACK + 1], EARLY, LATE)]
+        subtract_late(0, *picked[0])
+        early = quantise(grouped_d[1][:], EARLY, "d_1") + (0,)
+        subtract_late(1, *picked[1])
+        tags = (("bank_b", 2), ("bank_c", 2), ("bank_a", 3))
+        banks = [psum.tile([P, BANK], F32, name="y_%d" % n, tag=tags[n][0], bufs=tags[n][1]) for n in range(N_TILES)]
+        score(lambda n: banks[n], [mx_d[0], early], ((0, 256), (256, EARLY)), 0, EARLY)
+        picked.append(pick(h[PACK + 2], EARLY, LATE, held_after("d_1_grouped", [P, LATE], F32, "xa_late")))
+        picked.append(pick(h[PACK + 3], EARLY, LATE))
+        subtract_late(2, *picked[2])
+        subtract_late(3, *picked[3])
+
+        def finish_early(n):
+            finish(banks[n][:, :EARLY], EARLY, out[n * P : (n + 1) * P, :EARLY], "early_%d" % n)
+
+        finish_early(0)
+        grouped_late = round_change(diff_late, held_after("early_0_squared", [P, PACK * LATE], BF16, "d_late_grouped"))
+        finish_early(1)
+        finish_early(2)
+        late = quantise(grouped_late[:], LATE, "d_late") + (EARLY,)
+        bank_late = psum.tile([P, N_TILES, LATE], F32, name="bank_late")
+        score(lambda n: bank_late[:, n, :], [mx_d[0], late], ((EARLY, M),), EARLY, LATE)
+        finish(bank_late[:], LATE, out[:, EARLY:].rearrange("(n p) m -> p n m", p=P), "late")

@@ -164,7 +164,7 @@ def tile_list_octopus_pattern_change_kernel(
             bank_c = product("bank_c", 2, mx3[b][0][:, cols].bitcast(FP8X4), mx3[b][1][:, cols], hf)
             b_sb = ring.tile([P, BANK], F32, name="b_sb", bufs=3)
             nc.scalar.activation(out=b_sb[:], in_=bank_b[:], func=ACT.Copy)
-            most = ring.tile([P, BANK], F32, name="most", bufs=4)
+            most = held_after("most_%d" % hf, [P, BANK], F32, "most")
             nc.vector.tensor_tensor(out=most[:], in0=bank_c[:], in1=b_sb[:], op=ALU.max)
             return most
 
@@ -174,18 +174,16 @@ def tile_list_octopus_pattern_change_kernel(
             bank_a = product("bank_a", 3, mx1[b][0][:, cols].bitcast(FP8X4), mx1[b][1][:, cols], hf)
             nc.vector.tensor_tensor(out=h[:, hf * BANK : (hf + 1) * BANK], in0=bank_a[:], in1=most[:], op=ALU.mult)
 
-        def pick(h, m0, width, xa=None):
-            picked = []
-            for name, offsets, gain in (("xa", list2, gain_a), ("xb", list3, gain_b)):
-                x = xa if xa is not None and name == "xa" else ring.tile([P, width], F32, name=name, tag=name)
+        def pick(h, m0, xa, xb):
+            width = xa.shape[1]
+            for x, offsets, gain in ((xa, list2, gain_a), (xb, list3, gain_b)):
                 nc.vector.tensor_tensor(
                     out=x[:],
                     in0=h[:].indirect(offsets[:, m0 // 16 : (m0 + width) // 16]),
                     in1=gain[:, m0 : m0 + width],
                     op=ALU.mult,
                 )
-                picked.append(x)
-            return picked
+            return xa, xb
 
         def round_change(diff, grouped):
             nc.scalar.activation(
@@ -218,7 +216,7 @@ def tile_list_octopus_pattern_change_kernel(
             nc.scalar.activation(out=result[:], in_=squared[:], func=ACT.Ln, bias=1.0)
             nc.sync.dma_start(out=dst, in_=result[:])
 
-        h = [held([P, S], F32, "h_%d" % s) for s in range(SLICES)]
+        h = []
         widths = [M, EARLY]
         diff = [held([P, PACK, widths[b]], F32, "diff_%d" % b) for b in range(BLOCKS)]
         mx_d = []
@@ -228,6 +226,7 @@ def tile_list_octopus_pattern_change_kernel(
         for s in range(SLICES):
             b, i = divmod(s, PACK)
             most[s, 1] = larger(s, 1)
+            h.append(held_after("page_%d" % s, [P, S], F32, "h_%d" % s))
             feature(s, 0, most[s, 0], h[s])
             feature(s, 1, most[s, 1], h[s])
             if s == 1:
@@ -238,7 +237,9 @@ def tile_list_octopus_pattern_change_kernel(
                 mx_d.append(quantise(grouped_d[0][:], M, "d_0") + (0,))
             if s + 1 < SLICES:
                 most[s + 1, 0] = larger(s + 1, 0)
-            xa, xb = pick(h[s], 0, widths[b])
+            xa = held_after("xa", [P, widths[b]], F32, "xa")
+            xb = held_after("page_%d" % (s + 2), [P, widths[b]], F32, "xb")
+            pick(h[s], 0, xa, xb)
             (nc.gpsimd if s + 1 < SLICES else nc.vector).tensor_tensor(out=diff[b][:, i, :], in0=xa[:], in1=xb[:], op=ALU.subtract)
             if i == PACK - 1:
                 grouped_d.append(round_change(diff[b], held([P, PACK * widths[b]], BF16, "d_%d_grouped" % b)))
@@ -248,17 +249,21 @@ def tile_list_octopus_pattern_change_kernel(
         def subtract_late(i, xa, xb):
             nc.vector.tensor_tensor(out=diff_late[:, i, :], in0=xa[:], in1=xb[:], op=ALU.subtract)
 
-        picked = [pick(h[PACK], EARLY, LATE), pick(h[PACK + 1], EARLY, LATE)]
+        def pick_late(i, tag_a, tag_b):
+            xa = held_after(tag_a, [P, LATE], F32, "xa_late")
+            return pick(h[PACK + i], EARLY, xa, held_after(tag_b, [P, LATE], F32, "xb_late"))
+
+        picked = [pick_late(0, "most_0", "most_1"), pick_late(1, "xa", "page_%d" % (SLICES + 1))]
         subtract_late(0, *picked[0])
-        early = quantise(grouped_d[1][:], EARLY, "d_1") + (0,)
+        picked.append(pick_late(2, "most_0", "most_1"))
         subtract_late(1, *picked[1])
+        early = quantise(grouped_d[1][:], EARLY, "d_1") + (0,)
+        subtract_late(2, *picked[2])
         tags = (("bank_b", 2), ("bank_c", 2), ("bank_a", 3))
         banks = [psum.tile([P, BANK], F32, name="y_%d" % n, tag=tags[n][0], bufs=tags[n][1]) for n in range(N_TILES)]
         score(lambda n: banks[n], [mx_d[0], early], ((0, 256), (256, EARLY)), 0, EARLY)
-        picked.append(pick(h[PACK + 2], EARLY, LATE, held_after("d_1_grouped", [P, LATE], F32, "xa_late")))
-        picked.append(pick(h[PACK + 3], EARLY, LATE))
-        subtract_late(2, *picked[2])
-        subtract_late(3, *picked[3])
+        last = held_after("d_1_grouped", [P, 2, LATE], F32, "x_last")
+        subtract_late(3, *pick(h[SLICES - 1], EARLY, last[:, 0, :], last[:, 1, :]))
 
         def finish_early(n):
             finish(banks[n][:, :EARLY], EARLY, out[n * P : (n + 1) * P, :EARLY], "early_%d" % n)

@@ -56,12 +56,18 @@ def tile_list_octopus_pattern_change_kernel(
         list3 = keep.tile([P, M // 16], U16, name="list3")
         nc.sync.dma_start(list1[:], offs)
 
+        one = held([P, 1], F32, "one")
+        nc.vector.memset(one[:], 1.0)
+        unread = held([P, 1], F32, "unread")
+        nc.scalar.activation(out=unread[:], in_=one[:], func=ACT.Ln)
+
         table_scales = held([P, T], U8, "table_scales")
         nc.vector.memset(table_scales[:].bitcast(I32), 0)
         load_scale_rows(nc.scalar, table_scales[:].bitcast(I32), tab_scales[0].bitcast(I32))
         w2_plane = held([P, H], U8, "w2_plane")
-        nc.gpsimd.memset(w2_plane[:].bitcast(I32), 0)
-        load_scale_rows(nc.gpsimd, w2_plane[:].bitcast(I32), w2_scales[0].bitcast(I32))
+        for q in range(4):
+            rows = w2_scales[0, 4 * q : 4 * q + 4].bitcast(I32)
+            nc.sync.dma_start(out=w2_plane[32 * q : 32 * q + 32].bitcast(I32), in_=rows.partition_broadcast(8))
 
         w2_raw = held([P, 2 * H], U8, "w2_raw")
         nc.sync.dma_start(out=w2_raw[:].bitcast(I32), in_=w2_words[0].bitcast(I32))
@@ -74,8 +80,8 @@ def tile_list_octopus_pattern_change_kernel(
 
         def cast_weight(cast, grouped, raw, c0):
             width = raw.shape[2]
-            dealt = grouped[:].rearrange("p (i q j) -> p q j i", i=PACK, j=PACK)
-            cast(dealt[:, c0 // PACK : (c0 + width) // PACK], raw[:].rearrange("p j (q i) -> p q j i", i=PACK))
+            dealt = grouped[:].rearrange("p (i q j) -> p q i j", i=PACK, j=PACK)
+            cast(dealt[:, c0 // PACK : (c0 + width) // PACK], raw[:].rearrange("p j (q i) -> p q i j", i=PACK))
 
         def on_scalar(dst, src):
             nc.scalar.activation(out=dst, in_=src, func=ACT.Copy)
@@ -94,15 +100,15 @@ def tile_list_octopus_pattern_change_kernel(
         for b in range(BLOCKS):
             pairs = slice(2 * b * PASS, 2 * (b + 1) * PASS)
             nc.vector.tensor_copy(
-                out=w2_codes[:, pairs].rearrange("p (i q e) -> p q i e", i=PACK, e=2),
-                in_=w2_raw[:, pairs].rearrange("p (q i e) -> p q i e", i=PACK, e=2),
+                out=w2_codes[:, pairs].rearrange("p (i q e) -> p i q e", i=PACK, e=2),
+                in_=w2_raw[:, pairs].rearrange("p (q i e) -> p i q e", i=PACK, e=2),
             )
+        nc.vector.tensor_copy(
+            out=w2_dealt[:].rearrange("p (b i q) -> p b i q", b=BLOCKS, i=PACK),
+            in_=w2_plane[:].rearrange("p (b q i) -> p b i q", b=BLOCKS, i=PACK),
+        )
         v_scales = held([P, S], U8, "v_scales")
         nc.vector.tensor_copy(v_scales[:], table_scales[:].indirect(list1[:]))
-        nc.vector.tensor_copy(
-            out=w2_dealt[:].rearrange("p (b i q) -> p b q i", b=BLOCKS, i=PACK),
-            in_=w2_plane[:].rearrange("p (b q i) -> p b q i", b=BLOCKS, i=PACK),
-        )
 
         grouped3_0 = held([P, PACK * PASS], BF16, "grouped3_0")
         cast_weight(on_scalar, grouped3_0, raw3_0, 0)
@@ -187,27 +193,24 @@ def tile_list_octopus_pattern_change_kernel(
 
         def round_change(diff, grouped):
             nc.scalar.activation(
-                out=grouped[:].rearrange("p (c u i) -> p c i u", i=PACK, u=4),
-                in_=diff[:].rearrange("p i (c u) -> p c i u", u=4),
+                out=grouped[:].rearrange("p (m i) -> p m i", i=PACK),
+                in_=diff[:].rearrange("p i m -> p m i"),
                 func=ACT.Abs,
             )
             return grouped
 
-        def score(bank_of, mx_d, ranges, m0, width):
-            for n in range(N_TILES):
-                bank = bank_of(n)
-                for lo, hi in ranges:
-                    for b in range(BLOCKS):
-                        codes, scales, first = mx_d[b]
-                        nc.tensor.matmul_mx(
-                            out=bank[:, lo - m0 : hi - m0],
-                            lhsT=w4_codes[:, b, 2 * n * P : 2 * (n + 1) * P].bitcast(FP4X4),
-                            lhsT_scale=w4_plane[:, b, n * P : (n + 1) * P],
-                            rhs=codes[:, lo - first : hi - first].bitcast(FP8X4),
-                            rhs_scale=scales[:, lo - first : hi - first],
-                            start=(b == 0),
-                            stop=(b == BLOCKS - 1),
-                        )
+        def score(b, operand, first, targets):
+            codes, scales = operand
+            for n, lo, hi, y, opens, closes in targets:
+                nc.tensor.matmul_mx(
+                    out=y,
+                    lhsT=w4_codes[:, b, 2 * n * P : 2 * (n + 1) * P].bitcast(FP4X4),
+                    lhsT_scale=w4_plane[:, b, n * P : (n + 1) * P],
+                    rhs=codes[:, lo - first : hi - first].bitcast(FP8X4),
+                    rhs_scale=scales[:, lo - first : hi - first],
+                    start=(b == 0 and opens),
+                    stop=(b == BLOCKS - 1 and closes),
+                )
 
         def finish(y, width, dst, name):
             squared = held(list(y.shape), F32, name + "_squared")
@@ -234,7 +237,7 @@ def tile_list_octopus_pattern_change_kernel(
             if s == 2:
                 mx1.append(second_block(raw1_1, "w1_1"))
             if s == PACK + 1:
-                mx_d.append(quantise(grouped_d[0][:], M, "d_0") + (0,))
+                mx_d.append(quantise(grouped_d[0][:], M, "d_0"))
             if s + 1 < SLICES:
                 most[s + 1, 0] = larger(s + 1, 0)
             xa = held_after("xa", [P, widths[b]], F32, "xa")
@@ -243,6 +246,16 @@ def tile_list_octopus_pattern_change_kernel(
             (nc.gpsimd if s + 1 < SLICES else nc.vector).tensor_tensor(out=diff[b][:, i, :], in0=xa[:], in1=xb[:], op=ALU.subtract)
             if i == PACK - 1:
                 grouped_d.append(round_change(diff[b], held([P, PACK * widths[b]], BF16, "d_%d_grouped" % b)))
+
+        tags = (("bank_b", 2), ("bank_c", 2), ("bank_a", 3))
+        banks = [psum.tile([P, BANK], F32, name="y_%d" % n, tag=tags[n][0], bufs=tags[n][1]) for n in range(N_TILES)]
+        early_sums = [
+            (n, lo, hi, banks[n][:, lo:hi], lo == 0, hi == EARLY) for n in range(N_TILES) for lo, hi in ((0, 256), (256, EARLY))
+        ]
+        bank_late = psum.tile([P, N_TILES, LATE], F32, name="bank_late")
+        late_sums = [(n, EARLY, M, bank_late[:, n, :], n == 0, n == N_TILES - 1) for n in range(N_TILES)]
+        score(0, mx_d[0], 0, early_sums)
+        score(0, mx_d[0], 0, late_sums)
 
         diff_late = held([P, PACK, LATE], F32, "diff_late")
 
@@ -257,11 +270,9 @@ def tile_list_octopus_pattern_change_kernel(
         subtract_late(0, *picked[0])
         picked.append(pick_late(2, "most_0", "most_1"))
         subtract_late(1, *picked[1])
-        early = quantise(grouped_d[1][:], EARLY, "d_1") + (0,)
+        early = quantise(grouped_d[1][:], EARLY, "d_1")
         subtract_late(2, *picked[2])
-        tags = (("bank_b", 2), ("bank_c", 2), ("bank_a", 3))
-        banks = [psum.tile([P, BANK], F32, name="y_%d" % n, tag=tags[n][0], bufs=tags[n][1]) for n in range(N_TILES)]
-        score(lambda n: banks[n], [mx_d[0], early], ((0, 256), (256, EARLY)), 0, EARLY)
+        score(1, early, 0, early_sums)
         last = held_after("d_1_grouped", [P, 2, LATE], F32, "x_last")
         subtract_late(3, *pick(h[SLICES - 1], EARLY, last[:, 0, :], last[:, 1, :]))
 
@@ -272,7 +283,6 @@ def tile_list_octopus_pattern_change_kernel(
         grouped_late = round_change(diff_late, held_after("early_0_squared", [P, PACK * LATE], BF16, "d_late_grouped"))
         finish_early(1)
         finish_early(2)
-        late = quantise(grouped_late[:], LATE, "d_late") + (EARLY,)
-        bank_late = psum.tile([P, N_TILES, LATE], F32, name="bank_late")
-        score(lambda n: bank_late[:, n, :], [mx_d[0], late], ((EARLY, M),), EARLY, LATE)
+        late = quantise(grouped_late[:], LATE, "d_late")
+        score(1, late, EARLY, late_sums)
         finish(bank_late[:], LATE, out[:, EARLY:].rearrange("(n p) m -> p n m", p=P), "late")

@@ -81,7 +81,7 @@ def tile_list_octopus_pattern_change_kernel(
         def cast_weight(cast, grouped, raw, c0):
             width = raw.shape[2]
             dealt = grouped[:].rearrange("p (i q j) -> p q i j", i=PACK, j=PACK)
-            cast(dealt[:, c0 // PACK : (c0 + width) // PACK], raw[:].rearrange("p j (q i) -> p q i j", i=PACK))
+            cast(dealt[:, c0 // PACK : (c0 + width) // PACK], raw[:, :, :].rearrange("p j (q i) -> p q i j", i=PACK))
 
         def on_scalar(dst, src):
             nc.scalar.activation(out=dst, in_=src, func=ACT.Copy)
@@ -137,15 +137,13 @@ def tile_list_octopus_pattern_change_kernel(
         nc.sync.dma_start(out=raw3_1[:], in_=weight_rows(w3, PASS, PASS))
         raw1_1 = held_after("w2_raw", [P, PACK, PASS], F32, "raw1_1")
         nc.sync.dma_start(out=raw1_1[:], in_=weight_rows(w1, PASS, PASS))
-        w4_codes = held_after("w2_plane", [P, BLOCKS, 2 * N], U8, "w4_codes")
+        w4_codes = held_after("table_scales", [P, BLOCKS, 2 * N], U8, "w4_codes")
         nc.sync.dma_start(out=w4_codes[:].bitcast(I32), in_=w4_words.bitcast(I32).rearrange("b p n -> p b n"))
-        w4_plane = held_after("grouped1_0", [P, BLOCKS, N], U8, "w4_plane")
-        nc.gpsimd.memset(w4_plane[:].bitcast(I32), 0)
-        load_scale_rows(nc.sync, w4_plane[:].bitcast(I32), w4_scales.bitcast(I32).rearrange("b q n -> q b n"))
 
         def second_block(raw, name):
             grouped = held([P, PACK * PASS], BF16, "grouped" + name)
-            cast_weight(on_scalar, grouped, raw, 0)
+            for c0 in range(0, PASS, CHUNK):
+                cast_weight(on_scalar, grouped, raw[:, :, c0 : c0 + CHUNK], c0)
             return quantise(grouped[:], PASS, name)
 
         def product(tag, bufs, codes, scales, hf):
@@ -161,6 +159,8 @@ def tile_list_octopus_pattern_change_kernel(
             )
             return bank
 
+        most_tags = ("grouped1_0", "w2_plane")
+
         def larger(s, hf):
             b, i = divmod(s, PACK)
             cols = slice(i * P, (i + 1) * P)
@@ -168,9 +168,9 @@ def tile_list_octopus_pattern_change_kernel(
                 "bank_b", 2, w2_codes[:, 2 * s * P : 2 * (s + 1) * P].bitcast(FP4X4), w2_dealt[:, s * P : (s + 1) * P], hf
             )
             bank_c = product("bank_c", 2, mx3[b][0][:, cols].bitcast(FP8X4), mx3[b][1][:, cols], hf)
-            b_sb = ring.tile([P, BANK], F32, name="b_sb", bufs=3)
+            b_sb = ring.tile([P, BANK], F32, name="b_sb", bufs=4)
             nc.scalar.activation(out=b_sb[:], in_=bank_b[:], func=ACT.Copy)
-            most = held_after("most_%d" % hf, [P, BANK], F32, "most")
+            most = held_after(most_tags[hf], [P, BANK], F32, "most")
             nc.vector.tensor_tensor(out=most[:], in0=bank_c[:], in1=b_sb[:], op=ALU.max)
             return most
 
@@ -191,13 +191,12 @@ def tile_list_octopus_pattern_change_kernel(
                 )
             return xa, xb
 
-        def round_change(diff, grouped):
+        def round_change(diff, grouped, i0, i1):
             nc.scalar.activation(
-                out=grouped[:].rearrange("p (m i) -> p m i", i=PACK),
-                in_=diff[:].rearrange("p i m -> p m i"),
+                out=grouped[:].rearrange("p (m i) -> p m i", i=PACK)[:, :, i0:i1],
+                in_=diff[:, i0:i1, :].rearrange("p i m -> p m i"),
                 func=ACT.Abs,
             )
-            return grouped
 
         def score(b, operand, first, targets):
             codes, scales = operand
@@ -212,18 +211,21 @@ def tile_list_octopus_pattern_change_kernel(
                     stop=(b == BLOCKS - 1 and closes),
                 )
 
-        def finish(y, width, dst, name):
-            squared = held(list(y.shape), F32, name + "_squared")
+        def square(y, name):
+            squared = held(list(y.shape), F32, name)
             nc.scalar.activation(out=squared[:], in_=y, func=ACT.Square)
-            result = held(list(y.shape), F32, name + "_result")
+            return squared
+
+        def finish(squared, queue, dst, name):
+            result = held(list(squared.shape), F32, name)
             nc.scalar.activation(out=result[:], in_=squared[:], func=ACT.Ln, bias=1.0)
-            nc.sync.dma_start(out=dst, in_=result[:])
+            queue.dma_start(out=dst, in_=result[:])
 
         h = []
         widths = [M, EARLY]
         diff = [held([P, PACK, widths[b]], F32, "diff_%d" % b) for b in range(BLOCKS)]
         mx_d = []
-        grouped_d = []
+        grouped_d = [held([P, PACK * widths[b]], BF16, "d_%d_grouped" % b) for b in range(BLOCKS)]
 
         most = {(0, 0): larger(0, 0)}
         for s in range(SLICES):
@@ -236,6 +238,9 @@ def tile_list_octopus_pattern_change_kernel(
                 mx3.append(second_block(raw3_1, "w3_1"))
             if s == 2:
                 mx1.append(second_block(raw1_1, "w1_1"))
+                w4_plane = held_after("w2_raw", [P, BLOCKS, N], U8, "w4_plane")
+                nc.gpsimd.memset(w4_plane[:].bitcast(I32), 0)
+                load_scale_rows(nc.sync, w4_plane[:].bitcast(I32), w4_scales.bitcast(I32).rearrange("b q n -> q b n"))
             if s == PACK + 1:
                 mx_d.append(quantise(grouped_d[0][:], M, "d_0"))
             if s + 1 < SLICES:
@@ -244,8 +249,10 @@ def tile_list_octopus_pattern_change_kernel(
             xb = held_after("page_%d" % (s + 2), [P, widths[b]], F32, "xb")
             pick(h[s], 0, xa, xb)
             (nc.gpsimd if s + 1 < SLICES else nc.vector).tensor_tensor(out=diff[b][:, i, :], in0=xa[:], in1=xb[:], op=ALU.subtract)
-            if i == PACK - 1:
-                grouped_d.append(round_change(diff[b], held([P, PACK * widths[b]], BF16, "d_%d_grouped" % b)))
+            if s == PACK - 1:
+                round_change(diff[0], grouped_d[0], 0, PACK)
+            if b == 1 and i % 2 == 1:
+                round_change(diff[1], grouped_d[1], i - 1, i + 1)
 
         tags = (("bank_b", 2), ("bank_c", 2), ("bank_a", 3))
         banks = [psum.tile([P, BANK], F32, name="y_%d" % n, tag=tags[n][0], bufs=tags[n][1]) for n in range(N_TILES)]
@@ -266,23 +273,27 @@ def tile_list_octopus_pattern_change_kernel(
             xa = held_after(tag_a, [P, LATE], F32, "xa_late")
             return pick(h[PACK + i], EARLY, xa, held_after(tag_b, [P, LATE], F32, "xb_late"))
 
-        picked = [pick_late(0, "most_0", "most_1"), pick_late(1, "xa", "page_%d" % (SLICES + 1))]
+        def finish_early(n, squared):
+            finish(squared, nc.sync, out[n * P : (n + 1) * P, :EARLY], "result_%d" % n)
+
+        grouped_late = held([P, PACK * LATE], BF16, "d_late_grouped")
+        picked = [pick_late(0, *most_tags), pick_late(1, "xa", "page_%d" % (SLICES + 1))]
         subtract_late(0, *picked[0])
-        picked.append(pick_late(2, "most_0", "most_1"))
         subtract_late(1, *picked[1])
+        round_change(diff_late, grouped_late, 0, 2)
         early = quantise(grouped_d[1][:], EARLY, "d_1")
-        subtract_late(2, *picked[2])
         score(1, early, 0, early_sums)
-        last = held_after("d_1_grouped", [P, 2, LATE], F32, "x_last")
-        subtract_late(3, *pick(h[SLICES - 1], EARLY, last[:, 0, :], last[:, 1, :]))
+        last = held_after("d_1_grouped", [P, 2, 2, LATE], F32, "x_last")
+        picked = [pick(h[PACK + 2 + u], EARLY, last[:, u, 0, :], last[:, u, 1, :]) for u in range(2)]
+        subtract_late(2, *picked[0])
+        subtract_late(3, *picked[1])
 
-        def finish_early(n):
-            finish(banks[n][:, :EARLY], EARLY, out[n * P : (n + 1) * P, :EARLY], "early_%d" % n)
-
-        finish_early(0)
-        grouped_late = round_change(diff_late, held_after("early_0_squared", [P, PACK * LATE], BF16, "d_late_grouped"))
-        finish_early(1)
-        finish_early(2)
+        finish_early(0, square(banks[0][:, :EARLY], "squared_0"))
+        squared_1 = square(banks[1][:, :EARLY], "squared_1")
+        round_change(diff_late, grouped_late, 2, PACK)
         late = quantise(grouped_late[:], LATE, "d_late")
         score(1, late, EARLY, late_sums)
-        finish(bank_late[:], LATE, out[:, EARLY:].rearrange("(n p) m -> p n m", p=P), "late")
+        finish_early(1, squared_1)
+        finish_early(2, square(banks[2][:, :EARLY], "squared_2"))
+        squared_late = square(bank_late[:], "squared_late")
+        finish(squared_late, nc.sync, out[:, EARLY:].rearrange("(n p) m -> p n m", p=P), "result_late")

@@ -20,13 +20,19 @@ P = 128
 PACK = 4
 PASS = P * PACK
 BANK = 512
+GROUP = 16
+QUADRANT = 32
+SCALE_ROWS = 16
 HALVES = S // BANK
-BLOCKS = H // PASS
-SLICES = BLOCKS * PACK
+PASSES = H // PASS
+SLICES = PASSES * PACK
 N_TILES = N // P
-CHUNK = 256
+CHUNK = PASS // 2
 LATE = 128
 EARLY = M - LATE
+EARLY_RUNS = ((0, 256), (256, EARLY))
+BANK_B, BANK_C, BANK_A = ("bank_b", 2), ("bank_c", 2), ("bank_a", 3)
+B_COPIES = 4
 
 
 def tile_list_octopus_pattern_change_kernel(
@@ -35,25 +41,43 @@ def tile_list_octopus_pattern_change_kernel(
     nc = tc.nc
     with ExitStack() as ctx:
         keep = ctx.enter_context(tc.tile_pool(name="keep", bufs=1))
-        ring = ctx.enter_context(tc.tile_pool(name="ring", bufs=2))
+        ring = ctx.enter_context(tc.tile_pool(name="ring", bufs=B_COPIES))
         psum = ctx.enter_context(tc.psum_pool(name="psum", bufs=1))
 
         def held(shape, dtype, name):
             return keep.tile(shape, dtype, name=name, align_bytes=64)
 
-        def load_scale_rows(queue, plane, rows):
-            for r in range(4):
-                queue.dma_start(out=plane[r:P:32], in_=rows[r:16:4])
-
         def held_after(earlier, shape, dtype, name):
             return keep.tile(shape, dtype, name=name, tag=earlier, align_bytes=64)
+
+        def load_scale_rows(queue, plane, rows):
+            for r in range(4):
+                queue.dma_start(out=plane[r:P:QUADRANT], in_=rows[r:SCALE_ROWS:4])
 
         def weight_rows(w, c0, width):
             return w[:, c0 : c0 + width].rearrange("(p j) c -> p j c", j=PACK)
 
-        list1 = keep.tile([P, S // 16], U16, name="list1")
-        list2 = keep.tile([P, M // 16], U16, name="list2")
-        list3 = keep.tile([P, M // 16], U16, name="list3")
+        def round_weight(copy, grouped, raw, c0):
+            width = raw.shape[2]
+            dealt = grouped[:].rearrange("p (i q j) -> p q i j", i=PACK, j=PACK)
+            copy(dealt[:, c0 // PACK : (c0 + width) // PACK], raw[:, :, :].rearrange("p j (q i) -> p q i j", i=PACK))
+
+        def copy_on_scalar(dst, src):
+            nc.scalar.activation(out=dst, in_=src, func=ACT.Copy)
+
+        def copy_on_vector(dst, src):
+            nc.vector.tensor_copy(out=dst, in_=src)
+
+        def quantise(grouped, codes_after, name):
+            width = grouped.shape[1] // PACK
+            codes = held_after(codes_after, [P, width], U32, name + "_codes")
+            scales = held([P, width], U8, name + "_scales")
+            nc.vector.quantize_mx(out=codes[:].bitcast(FP8X4), scales=scales[:], in_=grouped[:])
+            return codes, scales
+
+        list1 = keep.tile([P, S // GROUP], U16, name="list1")
+        list2 = keep.tile([P, M // GROUP], U16, name="list2")
+        list3 = keep.tile([P, M // GROUP], U16, name="list3")
         nc.sync.dma_start(list1[:], offs)
 
         one = held([P, 1], F32, "one")
@@ -65,9 +89,11 @@ def tile_list_octopus_pattern_change_kernel(
         nc.vector.memset(table_scales[:].bitcast(I32), 0)
         load_scale_rows(nc.scalar, table_scales[:].bitcast(I32), tab_scales[0].bitcast(I32))
         w2_plane = held([P, H], U8, "w2_plane")
-        for q in range(4):
+        for q in range(P // QUADRANT):
             rows = w2_scales[0, 4 * q : 4 * q + 4].bitcast(I32)
-            nc.sync.dma_start(out=w2_plane[32 * q : 32 * q + 32].bitcast(I32), in_=rows.partition_broadcast(8))
+            nc.sync.dma_start(
+                out=w2_plane[QUADRANT * q : QUADRANT * (q + 1)].bitcast(I32), in_=rows.partition_broadcast(QUADRANT // 4)
+            )
 
         w2_raw = held([P, 2 * H], U8, "w2_raw")
         nc.sync.dma_start(out=w2_raw[:].bitcast(I32), in_=w2_words[0].bitcast(I32))
@@ -78,41 +104,24 @@ def tile_list_octopus_pattern_change_kernel(
         table = held([P, T], U32, "table")
         nc.sync.dma_start(out=table[:].bitcast(I32), in_=tab_words[0].rearrange("p t i -> p (t i)").bitcast(I32))
 
-        def cast_weight(cast, grouped, raw, c0):
-            width = raw.shape[2]
-            dealt = grouped[:].rearrange("p (i q j) -> p q i j", i=PACK, j=PACK)
-            cast(dealt[:, c0 // PACK : (c0 + width) // PACK], raw[:, :, :].rearrange("p j (q i) -> p q i j", i=PACK))
-
-        def on_scalar(dst, src):
-            nc.scalar.activation(out=dst, in_=src, func=ACT.Copy)
-
-        def on_vector(dst, src):
-            nc.vector.tensor_copy(out=dst, in_=src)
-
-        def quantise(grouped, width, name):
-            codes = held([P, width], U32, name + "_codes")
-            scales = held([P, width], U8, name + "_scales")
-            nc.vector.quantize_mx(out=codes[:].bitcast(FP8X4), scales=scales[:], in_=grouped)
-            return codes, scales
-
         w2_codes = held([P, 2 * H], U8, "w2_codes")
         w2_dealt = held([P, H], U8, "w2_dealt")
-        for b in range(BLOCKS):
+        for b in range(PASSES):
             pairs = slice(2 * b * PASS, 2 * (b + 1) * PASS)
             nc.vector.tensor_copy(
                 out=w2_codes[:, pairs].rearrange("p (i q e) -> p i q e", i=PACK, e=2),
                 in_=w2_raw[:, pairs].rearrange("p (q i e) -> p i q e", i=PACK, e=2),
             )
         nc.vector.tensor_copy(
-            out=w2_dealt[:].rearrange("p (b i q) -> p b i q", b=BLOCKS, i=PACK),
-            in_=w2_plane[:].rearrange("p (b q i) -> p b i q", b=BLOCKS, i=PACK),
+            out=w2_dealt[:].rearrange("p (b i q) -> p b i q", b=PASSES, i=PACK),
+            in_=w2_plane[:].rearrange("p (b q i) -> p b i q", b=PASSES, i=PACK),
         )
         v_scales = held([P, S], U8, "v_scales")
         nc.vector.tensor_copy(v_scales[:], table_scales[:].indirect(list1[:]))
 
         grouped3_0 = held([P, PACK * PASS], BF16, "grouped3_0")
-        cast_weight(on_scalar, grouped3_0, raw3_0, 0)
-        mx3 = [quantise(grouped3_0[:], PASS, "w3_0")]
+        round_weight(copy_on_scalar, grouped3_0, raw3_0, 0)
+        mx3 = [quantise(grouped3_0, "w3_0_codes", "w3_0")]
 
         raw1_0a = held_after("w2_raw", [P, PACK, CHUNK], F32, "raw1_0a")
         nc.sync.dma_start(out=raw1_0a[:], in_=weight_rows(w1, 0, CHUNK))
@@ -126,27 +135,28 @@ def tile_list_octopus_pattern_change_kernel(
         v_words = []
         for hf in range(HALVES):
             words = held([P, BANK], U32, "v_words_%d" % hf)
-            nc.vector.tensor_copy(words[:], table[:].indirect(list1[:, hf * BANK // 16 : (hf + 1) * BANK // 16]))
+            nc.vector.tensor_copy(words[:], table[:].indirect(list1[:, hf * BANK // GROUP : (hf + 1) * BANK // GROUP]))
             v_words.append(words)
         grouped1_0 = held([P, PACK * PASS], BF16, "grouped1_0")
-        cast_weight(on_scalar, grouped1_0, raw1_0a, 0)
-        cast_weight(on_vector, grouped1_0, raw1_0b, CHUNK)
-        mx1 = [quantise(grouped1_0[:], PASS, "w1_0")]
+        round_weight(copy_on_scalar, grouped1_0, raw1_0a, 0)
+        round_weight(copy_on_vector, grouped1_0, raw1_0b, CHUNK)
+        mx1 = [quantise(grouped1_0, "w1_0_codes", "w1_0")]
 
         raw3_1 = held_after("table", [P, PACK, PASS], F32, "raw3_1")
         nc.sync.dma_start(out=raw3_1[:], in_=weight_rows(w3, PASS, PASS))
         raw1_1 = held_after("w2_raw", [P, PACK, PASS], F32, "raw1_1")
         nc.sync.dma_start(out=raw1_1[:], in_=weight_rows(w1, PASS, PASS))
-        w4_codes = held_after("table_scales", [P, BLOCKS, 2 * N], U8, "w4_codes")
+        w4_codes = held_after("table_scales", [P, PASSES, 2 * N], U8, "w4_codes")
         nc.sync.dma_start(out=w4_codes[:].bitcast(I32), in_=w4_words.bitcast(I32).rearrange("b p n -> p b n"))
 
-        def second_block(raw, name):
-            grouped = held([P, PACK * PASS], BF16, "grouped" + name)
+        def round_second_pass(raw, name):
+            grouped = held([P, PACK * PASS], BF16, name)
             for c0 in range(0, PASS, CHUNK):
-                cast_weight(on_scalar, grouped, raw[:, :, c0 : c0 + CHUNK], c0)
-            return quantise(grouped[:], PASS, name)
+                round_weight(copy_on_scalar, grouped, raw[:, :, c0 : c0 + CHUNK], c0)
+            return grouped
 
-        def product(tag, bufs, codes, scales, hf):
+        def product(bank_kind, codes, scales, hf):
+            tag, bufs = bank_kind
             bank = psum.tile([P, BANK], F32, name=tag, tag=tag, bufs=bufs)
             nc.tensor.matmul_mx(
                 out=bank[:],
@@ -165,27 +175,27 @@ def tile_list_octopus_pattern_change_kernel(
             b, i = divmod(s, PACK)
             cols = slice(i * P, (i + 1) * P)
             bank_b = product(
-                "bank_b", 2, w2_codes[:, 2 * s * P : 2 * (s + 1) * P].bitcast(FP4X4), w2_dealt[:, s * P : (s + 1) * P], hf
+                BANK_B, w2_codes[:, 2 * s * P : 2 * (s + 1) * P].bitcast(FP4X4), w2_dealt[:, s * P : (s + 1) * P], hf
             )
-            bank_c = product("bank_c", 2, mx3[b][0][:, cols].bitcast(FP8X4), mx3[b][1][:, cols], hf)
-            b_sb = ring.tile([P, BANK], F32, name="b_sb", bufs=4)
-            nc.scalar.activation(out=b_sb[:], in_=bank_b[:], func=ACT.Copy)
+            bank_c = product(BANK_C, mx3[b][0][:, cols].bitcast(FP8X4), mx3[b][1][:, cols], hf)
+            b_copy = ring.tile([P, BANK], F32, name="b_copy")
+            copy_on_scalar(b_copy[:], bank_b[:])
             most = held_after(most_tags[hf], [P, BANK], F32, "most")
-            nc.vector.tensor_tensor(out=most[:], in0=bank_c[:], in1=b_sb[:], op=ALU.max)
+            nc.vector.tensor_tensor(out=most[:], in0=bank_c[:], in1=b_copy[:], op=ALU.max)
             return most
 
-        def feature(s, hf, most, h):
+        def feature(s, hf, most, h_slice):
             b, i = divmod(s, PACK)
             cols = slice(i * P, (i + 1) * P)
-            bank_a = product("bank_a", 3, mx1[b][0][:, cols].bitcast(FP8X4), mx1[b][1][:, cols], hf)
-            nc.vector.tensor_tensor(out=h[:, hf * BANK : (hf + 1) * BANK], in0=bank_a[:], in1=most[:], op=ALU.mult)
+            bank_a = product(BANK_A, mx1[b][0][:, cols].bitcast(FP8X4), mx1[b][1][:, cols], hf)
+            nc.vector.tensor_tensor(out=h_slice[:, hf * BANK : (hf + 1) * BANK], in0=bank_a[:], in1=most[:], op=ALU.mult)
 
-        def pick(h, m0, xa, xb):
+        def pick(h_slice, m0, xa, xb):
             width = xa.shape[1]
             for x, offsets, gain in ((xa, list2, gain_a), (xb, list3, gain_b)):
                 nc.vector.tensor_tensor(
                     out=x[:],
-                    in0=h[:].indirect(offsets[:, m0 // 16 : (m0 + width) // 16]),
+                    in0=h_slice[:].indirect(offsets[:, m0 // GROUP : (m0 + width) // GROUP]),
                     in1=gain[:, m0 : m0 + width],
                     op=ALU.mult,
                 )
@@ -198,35 +208,11 @@ def tile_list_octopus_pattern_change_kernel(
                 func=ACT.Abs,
             )
 
-        def score(b, operand, first, targets):
-            codes, scales = operand
-            for n, lo, hi, y, opens, closes in targets:
-                nc.tensor.matmul_mx(
-                    out=y,
-                    lhsT=w4_codes[:, b, 2 * n * P : 2 * (n + 1) * P].bitcast(FP4X4),
-                    lhsT_scale=w4_plane[:, b, n * P : (n + 1) * P],
-                    rhs=codes[:, lo - first : hi - first].bitcast(FP8X4),
-                    rhs_scale=scales[:, lo - first : hi - first],
-                    start=(b == 0 and opens),
-                    stop=(b == BLOCKS - 1 and closes),
-                )
-
-        def square(y, name):
-            squared = held(list(y.shape), F32, name)
-            nc.scalar.activation(out=squared[:], in_=y, func=ACT.Square)
-            return squared
-
-        def finish(squared, queue, dst, name):
-            result = held(list(squared.shape), F32, name)
-            nc.scalar.activation(out=result[:], in_=squared[:], func=ACT.Ln, bias=1.0)
-            queue.dma_start(out=dst, in_=result[:])
-
-        h = []
         widths = [M, EARLY]
-        diff = [held([P, PACK, widths[b]], F32, "diff_%d" % b) for b in range(BLOCKS)]
-        mx_d = []
-        grouped_d = [held([P, PACK * widths[b]], BF16, "d_%d_grouped" % b) for b in range(BLOCKS)]
-
+        diff = [held([P, PACK, widths[b]], F32, "diff_%d" % b) for b in range(PASSES)]
+        grouped_d = [held([P, PACK * widths[b]], BF16, "grouped_d_%d" % b) for b in range(PASSES)]
+        h = []
+        xa_tag = "xa"
         most = {(0, 0): larger(0, 0)}
         for s in range(SLICES):
             b, i = divmod(s, PACK)
@@ -234,37 +220,72 @@ def tile_list_octopus_pattern_change_kernel(
             h.append(held_after("page_%d" % s, [P, S], F32, "h_%d" % s))
             feature(s, 0, most[s, 0], h[s])
             feature(s, 1, most[s, 1], h[s])
-            if s == 1:
-                mx3.append(second_block(raw3_1, "w3_1"))
-            if s == 2:
-                mx1.append(second_block(raw1_1, "w1_1"))
-                w4_plane = held_after("w2_raw", [P, BLOCKS, N], U8, "w4_plane")
+            if s == PACK - 3:
+                grouped3_1 = round_second_pass(raw3_1, "grouped3_1")
+            if s == PACK - 2:
+                grouped1_1 = round_second_pass(raw1_1, "grouped1_1")
+                w4_plane = held_after("w2_raw", [P, PASSES, N], U8, "w4_plane")
                 nc.gpsimd.memset(w4_plane[:].bitcast(I32), 0)
                 load_scale_rows(nc.sync, w4_plane[:].bitcast(I32), w4_scales.bitcast(I32).rearrange("b q n -> q b n"))
-            if s == PACK + 1:
-                mx_d.append(quantise(grouped_d[0][:], M, "d_0"))
             if s + 1 < SLICES:
                 most[s + 1, 0] = larger(s + 1, 0)
-            xa = held_after("xa", [P, widths[b]], F32, "xa")
+            if s == PACK - 2:
+                mx3.append(quantise(grouped3_1, xa_tag, "w3_1"))
+                xa_tag = "grouped3_1"
+            if s == PACK - 1:
+                mx1.append(quantise(grouped1_1, xa_tag, "w1_1"))
+                xa_tag = "grouped1_1"
+            if s == PACK + 1:
+                mx_d0 = quantise(grouped_d[0], xa_tag, "d_0")
+                xa_tag = "grouped_d_0"
+            xa = held_after(xa_tag, [P, widths[b]], F32, "xa")
             xb = held_after("page_%d" % (s + 2), [P, widths[b]], F32, "xb")
             pick(h[s], 0, xa, xb)
-            (nc.gpsimd if s + 1 < SLICES else nc.vector).tensor_tensor(out=diff[b][:, i, :], in0=xa[:], in1=xb[:], op=ALU.subtract)
+            subtracts = nc.gpsimd if s + 1 < SLICES else nc.vector
+            subtracts.tensor_tensor(out=diff[b][:, i, :], in0=xa[:], in1=xb[:], op=ALU.subtract)
             if s == PACK - 1:
                 round_change(diff[0], grouped_d[0], 0, PACK)
             if b == 1 and i % 2 == 1:
                 round_change(diff[1], grouped_d[1], i - 1, i + 1)
 
-        tags = (("bank_b", 2), ("bank_c", 2), ("bank_a", 3))
-        banks = [psum.tile([P, BANK], F32, name="y_%d" % n, tag=tags[n][0], bufs=tags[n][1]) for n in range(N_TILES)]
-        early_sums = [
-            (n, lo, hi, banks[n][:, lo:hi], lo == 0, hi == EARLY) for n in range(N_TILES) for lo, hi in ((0, 256), (256, EARLY))
+        def score(b, operand, first, sums):
+            codes, scales = operand
+            for n, lo, hi, y, opens, closes in sums:
+                nc.tensor.matmul_mx(
+                    out=y,
+                    lhsT=w4_codes[:, b, 2 * n * P : 2 * (n + 1) * P].bitcast(FP4X4),
+                    lhsT_scale=w4_plane[:, b, n * P : (n + 1) * P],
+                    rhs=codes[:, lo - first : hi - first].bitcast(FP8X4),
+                    rhs_scale=scales[:, lo - first : hi - first],
+                    start=(b == 0 and opens),
+                    stop=(b == PASSES - 1 and closes),
+                )
+
+        def square(y, name):
+            squared = held(list(y.shape), F32, name)
+            nc.scalar.activation(out=squared[:], in_=y, func=ACT.Square)
+            return squared
+
+        def finish(squared, dst, name):
+            result = held(list(squared.shape), F32, name)
+            nc.scalar.activation(out=result[:], in_=squared[:], func=ACT.Ln, bias=1.0)
+            nc.sync.dma_start(out=dst, in_=result[:])
+
+        def finish_early(n, squared):
+            finish(squared, out[n * P : (n + 1) * P, :EARLY], "result_%d" % n)
+
+        banks = [
+            psum.tile([P, BANK], F32, name="y_%d" % n, tag=tag, bufs=bufs)
+            for n, (tag, bufs) in enumerate((BANK_B, BANK_C, BANK_A))
         ]
+        early_sums = [(n, lo, hi, banks[n][:, lo:hi], lo == 0, hi == EARLY) for n in range(N_TILES) for lo, hi in EARLY_RUNS]
         bank_late = psum.tile([P, N_TILES, LATE], F32, name="bank_late")
         late_sums = [(n, EARLY, M, bank_late[:, n, :], n == 0, n == N_TILES - 1) for n in range(N_TILES)]
-        score(0, mx_d[0], 0, early_sums)
-        score(0, mx_d[0], 0, late_sums)
+        score(0, mx_d0, 0, early_sums)
+        score(0, mx_d0, 0, late_sums)
 
         diff_late = held([P, PACK, LATE], F32, "diff_late")
+        grouped_late = held([P, PACK * LATE], BF16, "grouped_late")
 
         def subtract_late(i, xa, xb):
             nc.vector.tensor_tensor(out=diff_late[:, i, :], in0=xa[:], in1=xb[:], op=ALU.subtract)
@@ -273,17 +294,12 @@ def tile_list_octopus_pattern_change_kernel(
             xa = held_after(tag_a, [P, LATE], F32, "xa_late")
             return pick(h[PACK + i], EARLY, xa, held_after(tag_b, [P, LATE], F32, "xb_late"))
 
-        def finish_early(n, squared):
-            finish(squared, nc.sync, out[n * P : (n + 1) * P, :EARLY], "result_%d" % n)
-
-        grouped_late = held([P, PACK * LATE], BF16, "d_late_grouped")
-        picked = [pick_late(0, *most_tags), pick_late(1, "xa", "page_%d" % (SLICES + 1))]
+        picked = [pick_late(0, "page_%d" % SLICES, most_tags[1]), pick_late(1, xa_tag, "page_%d" % (SLICES + 1))]
         subtract_late(0, *picked[0])
         subtract_late(1, *picked[1])
         round_change(diff_late, grouped_late, 0, 2)
-        early = quantise(grouped_d[1][:], EARLY, "d_1")
-        score(1, early, 0, early_sums)
-        last = held_after("d_1_grouped", [P, 2, 2, LATE], F32, "x_last")
+        score(1, quantise(grouped_d[1], "d_1_codes", "d_1"), 0, early_sums)
+        last = held_after("grouped_d_1", [P, 2, 2, LATE], F32, "x_last")
         picked = [pick(h[PACK + 2 + u], EARLY, last[:, u, 0, :], last[:, u, 1, :]) for u in range(2)]
         subtract_late(2, *picked[0])
         subtract_late(3, *picked[1])
@@ -291,9 +307,7 @@ def tile_list_octopus_pattern_change_kernel(
         finish_early(0, square(banks[0][:, :EARLY], "squared_0"))
         squared_1 = square(banks[1][:, :EARLY], "squared_1")
         round_change(diff_late, grouped_late, 2, PACK)
-        late = quantise(grouped_late[:], LATE, "d_late")
-        score(1, late, EARLY, late_sums)
+        score(1, quantise(grouped_late, "d_late_codes", "d_late"), EARLY, late_sums)
         finish_early(1, squared_1)
         finish_early(2, square(banks[2][:, :EARLY], "squared_2"))
-        squared_late = square(bank_late[:], "squared_late")
-        finish(squared_late, nc.sync, out[:, EARLY:].rearrange("(n p) m -> p n m", p=P), "result_late")
+        finish(square(bank_late[:], "squared_late"), out[:, EARLY:].rearrange("(n p) m -> p n m", p=P), "result_late")

from contextlib import ExitStack

import concourse.mybir as mybir

K, H, N, T, S, M = 512, 1024, 384, 4096, 1024, 512
FLOPS = 3 * 2 * K * H * S + 2 * H * N * M

F32 = mybir.dt.float32
BF16 = mybir.dt.bfloat16
I32 = mybir.dt.int32
U32 = mybir.dt.uint32
U16 = mybir.dt.uint16
U8 = mybir.dt.uint8
FP8X4 = mybir.dt.float8_e4m3fn_x4
FP4X4 = mybir.dt.float4_e2m1fn_x4
ALU = mybir.AluOpType
ACT = mybir.ActivationFunctionType

P = 128
PACK = 4
PASS = P * PACK
BANK = 512
GROUP = 16
QUADRANT = 32
SCALE_ROWS = 16
HALVES = S // BANK
PASSES = H // PASS
SLICES = PASSES * PACK
N_TILES = N // P
CHUNK = PASS // 2
LATE = 128
EARLY = M - LATE
EARLY_RUNS = ((0, 256), (256, EARLY))
BANK_B, BANK_C, BANK_A = ("bank_b", 2), ("bank_c", 2), ("bank_a", 3)
B_COPIES = 4


def tile_list_octopus_pattern_change_kernel(
    tc, tab_words, tab_scales, w1, w2_words, w2_scales, w3, w4_words, w4_scales, wga, wgb, offs, offs2, offs3, out
):
    nc = tc.nc
    with ExitStack() as ctx:
        keep = ctx.enter_context(tc.tile_pool(name="keep", bufs=1))
        ring = ctx.enter_context(tc.tile_pool(name="ring", bufs=B_COPIES))
        psum = ctx.enter_context(tc.psum_pool(name="psum", bufs=1))

        def held(shape, dtype, name):
            return keep.tile(shape, dtype, name=name, align_bytes=64)

        def held_after(earlier, shape, dtype, name):
            return keep.tile(shape, dtype, name=name, tag=earlier, align_bytes=64)

        def load_scale_rows(queue, plane, rows):
            for r in range(4):
                queue.dma_start(out=plane[r:P:QUADRANT], in_=rows[r:SCALE_ROWS:4])

        def weight_rows(w, c0, width):
            return w[:, c0 : c0 + width].rearrange("(p j) c -> p j c", j=PACK)

        def round_weight(copy, grouped, raw, c0):
            width = raw.shape[2]
            dealt = grouped[:].rearrange("p (i q j) -> p q i j", i=PACK, j=PACK)
            copy(dealt[:, c0 // PACK : (c0 + width) // PACK], raw[:, :, :].rearrange("p j (q i) -> p q i j", i=PACK))

        def copy_on_scalar(dst, src):
            nc.scalar.activation(out=dst, in_=src, func=ACT.Copy)

        def copy_on_vector(dst, src):
            nc.vector.tensor_copy(out=dst, in_=src)

        def quantise(grouped, codes_after, name):
            width = grouped.shape[1] // PACK
            codes = held_after(codes_after, [P, width], U32, name + "_codes")
            scales = held([P, width], U8, name + "_scales")
            nc.vector.quantize_mx(out=codes[:].bitcast(FP8X4), scales=scales[:], in_=grouped[:])
            return codes, scales

        list1 = keep.tile([P, S // GROUP], U16, name="list1")
        list2 = keep.tile([P, M // GROUP], U16, name="list2")
        list3 = keep.tile([P, M // GROUP], U16, name="list3")
        nc.sync.dma_start(list1[:], offs)

        one = held([P, 1], F32, "one")
        nc.vector.memset(one[:], 1.0)
        unread = held([P, 1], F32, "unread")
        nc.scalar.activation(out=unread[:], in_=one[:], func=ACT.Ln)

        table_scales = held([P, T], U8, "table_scales")
        nc.vector.memset(table_scales[:].bitcast(I32), 0)
        load_scale_rows(nc.scalar, table_scales[:].bitcast(I32), tab_scales[0].bitcast(I32))
        w2_plane = held([P, H], U8, "w2_plane")
        for q in range(P // QUADRANT):
            rows = w2_scales[0, 4 * q : 4 * q + 4].bitcast(I32)
            nc.sync.dma_start(
                out=w2_plane[QUADRANT * q : QUADRANT * (q + 1)].bitcast(I32), in_=rows.partition_broadcast(QUADRANT // 4)
            )

        w2_raw = held([P, 2 * H], U8, "w2_raw")
        nc.sync.dma_start(out=w2_raw[:].bitcast(I32), in_=w2_words[0].bitcast(I32))
        raw3_0 = held([P, PACK, PASS], F32, "raw3_0")
        nc.sync.dma_start(out=raw3_0[:], in_=weight_rows(w3, 0, PASS))
        nc.sync.dma_start(list2[:], offs2)
        nc.sync.dma_start(list3[:], offs3)
        table = held([P, T], U32, "table")
        nc.sync.dma_start(out=table[:].bitcast(I32), in_=tab_words[0].rearrange("p t i -> p (t i)").bitcast(I32))

        w2_codes = held([P, 2 * H], U8, "w2_codes")
        w2_dealt = held([P, H], U8, "w2_dealt")
        for b in range(PASSES):
            pairs = slice(2 * b * PASS, 2 * (b + 1) * PASS)
            nc.vector.tensor_copy(
                out=w2_codes[:, pairs].rearrange("p (i q e) -> p i q e", i=PACK, e=2),
                in_=w2_raw[:, pairs].rearrange("p (q i e) -> p i q e", i=PACK, e=2),
            )
        nc.vector.tensor_copy(
            out=w2_dealt[:].rearrange("p (b i q) -> p b i q", b=PASSES, i=PACK),
            in_=w2_plane[:].rearrange("p (b q i) -> p b i q", b=PASSES, i=PACK),
        )
        v_scales = held([P, S], U8, "v_scales")
        nc.vector.tensor_copy(v_scales[:], table_scales[:].indirect(list1[:]))

        grouped3_0 = held([P, PACK * PASS], BF16, "grouped3_0")
        round_weight(copy_on_scalar, grouped3_0, raw3_0, 0)
        mx3 = [quantise(grouped3_0, "w3_0_codes", "w3_0")]

        raw1_0a = held_after("w2_raw", [P, PACK, CHUNK], F32, "raw1_0a")
        nc.sync.dma_start(out=raw1_0a[:], in_=weight_rows(w1, 0, CHUNK))
        raw1_0b = held_after("w2_plane", [P, PACK, CHUNK], F32, "raw1_0b")
        nc.sync.dma_start(out=raw1_0b[:], in_=weight_rows(w1, CHUNK, CHUNK))
        gains = held_after("raw3_0", [P, 2, M], F32, "gains")
        gain_a, gain_b = gains[:, 0, :], gains[:, 1, :]
        nc.sync.dma_start(out=gain_a, in_=wga)
        nc.sync.dma_start(out=gain_b, in_=wgb)

        v_words = []
        for hf in range(HALVES):
            words = held([P, BANK], U32, "v_words_%d" % hf)
            nc.vector.tensor_copy(words[:], table[:].indirect(list1[:, hf * BANK // GROUP : (hf + 1) * BANK // GROUP]))
            v_words.append(words)
        grouped1_0 = held([P, PACK * PASS], BF16, "grouped1_0")
        round_weight(copy_on_scalar, grouped1_0, raw1_0a, 0)
        round_weight(copy_on_vector, grouped1_0, raw1_0b, CHUNK)
        mx1 = [quantise(grouped1_0, "w1_0_codes", "w1_0")]

        raw3_1 = held_after("table", [P, PACK, PASS], F32, "raw3_1")
        nc.sync.dma_start(out=raw3_1[:], in_=weight_rows(w3, PASS, PASS))
        raw1_1 = held_after("w2_raw", [P, PACK, PASS], F32, "raw1_1")
        nc.sync.dma_start(out=raw1_1[:], in_=weight_rows(w1, PASS, PASS))
        w4_codes = held_after("table_scales", [P, PASSES, 2 * N], U8, "w4_codes")
        nc.sync.dma_start(out=w4_codes[:].bitcast(I32), in_=w4_words.bitcast(I32).rearrange("b p n -> p b n"))

        def round_second_pass(raw, name):
            grouped = held([P, PACK * PASS], BF16, name)
            for c0 in range(0, PASS, CHUNK):
                round_weight(copy_on_scalar, grouped, raw[:, :, c0 : c0 + CHUNK], c0)
            return grouped

        def product(bank_kind, codes, scales, hf):
            tag, bufs = bank_kind
            bank = psum.tile([P, BANK], F32, name=tag, tag=tag, bufs=bufs)
            nc.tensor.matmul_mx(
                out=bank[:],
                lhsT=codes,
                lhsT_scale=scales,
                rhs=v_words[hf][:].bitcast(FP8X4),
                rhs_scale=v_scales[:, hf * BANK : (hf + 1) * BANK],
                start=True,
                stop=True,
            )
            return bank

        most_tags = ("grouped1_0", "w2_plane")

        def larger(s, hf):
            b, i = divmod(s, PACK)
            cols = slice(i * P, (i + 1) * P)
            bank_b = product(
                BANK_B, w2_codes[:, 2 * s * P : 2 * (s + 1) * P].bitcast(FP4X4), w2_dealt[:, s * P : (s + 1) * P], hf
            )
            bank_c = product(BANK_C, mx3[b][0][:, cols].bitcast(FP8X4), mx3[b][1][:, cols], hf)
            b_copy = ring.tile([P, BANK], F32, name="b_copy")
            copy_on_scalar(b_copy[:], bank_b[:])
            most = held_after(most_tags[hf], [P, BANK], F32, "most")
            nc.vector.tensor_tensor(out=most[:], in0=bank_c[:], in1=b_copy[:], op=ALU.max)
            return most

        def feature(s, hf, most, h_slice):
            b, i = divmod(s, PACK)
            cols = slice(i * P, (i + 1) * P)
            bank_a = product(BANK_A, mx1[b][0][:, cols].bitcast(FP8X4), mx1[b][1][:, cols], hf)
            nc.vector.tensor_tensor(out=h_slice[:, hf * BANK : (hf + 1) * BANK], in0=bank_a[:], in1=most[:], op=ALU.mult)

        def pick(h_slice, m0, xa, xb):
            width = xa.shape[1]
            for x, offsets, gain in ((xa, list2, gain_a), (xb, list3, gain_b)):
                nc.vector.tensor_tensor(
                    out=x[:],
                    in0=h_slice[:].indirect(offsets[:, m0 // GROUP : (m0 + width) // GROUP]),
                    in1=gain[:, m0 : m0 + width],
                    op=ALU.mult,
                )
            return xa, xb

        def round_change(diff, grouped, i0, i1):
            nc.scalar.activation(
                out=grouped[:].rearrange("p (m i) -> p m i", i=PACK)[:, :, i0:i1],
                in_=diff[:, i0:i1, :].rearrange("p i m -> p m i"),
                func=ACT.Abs,
            )

        widths = [M, EARLY]
        diff = [held([P, PACK, widths[b]], F32, "diff_%d" % b) for b in range(PASSES)]
        grouped_d = [held([P, PACK * widths[b]], BF16, "grouped_d_%d" % b) for b in range(PASSES)]
        h = []
        xa_tag = "xa"
        most = {(0, 0): larger(0, 0)}
        for s in range(SLICES):
            b, i = divmod(s, PACK)
            most[s, 1] = larger(s, 1)
            h.append(held_after("page_%d" % s, [P, S], F32, "h_%d" % s))
            feature(s, 0, most[s, 0], h[s])
            feature(s, 1, most[s, 1], h[s])
            if s == PACK - 3:
                grouped3_1 = round_second_pass(raw3_1, "grouped3_1")
            if s == PACK - 2:
                grouped1_1 = round_second_pass(raw1_1, "grouped1_1")
                w4_plane = held_after("w2_raw", [P, PASSES, N], U8, "w4_plane")
                nc.gpsimd.memset(w4_plane[:].bitcast(I32), 0)
                load_scale_rows(nc.sync, w4_plane[:].bitcast(I32), w4_scales.bitcast(I32).rearrange("b q n -> q b n"))
            if s + 1 < SLICES:
                most[s + 1, 0] = larger(s + 1, 0)
            if s == PACK - 2:
                mx3.append(quantise(grouped3_1, xa_tag, "w3_1"))
                xa_tag = "grouped3_1"
            if s == PACK - 1:
                mx1.append(quantise(grouped1_1, xa_tag, "w1_1"))
                xa_tag = "grouped1_1"
            if s == PACK + 1:
                mx_d0 = quantise(grouped_d[0], xa_tag, "d_0")
                xa_tag = "grouped_d_0"
            xa = held_after(xa_tag, [P, widths[b]], F32, "xa")
            xb = held_after("page_%d" % (s + 2), [P, widths[b]], F32, "xb")
            pick(h[s], 0, xa, xb)
            subtracts = nc.gpsimd if s + 1 < SLICES else nc.vector
            subtracts.tensor_tensor(out=diff[b][:, i, :], in0=xa[:], in1=xb[:], op=ALU.subtract)
            if s == PACK - 1:
                round_change(diff[0], grouped_d[0], 0, PACK)
            if b == 1 and i % 2 == 1:
                round_change(diff[1], grouped_d[1], i - 1, i + 1)

        def score(b, operand, first, sums):
            codes, scales = operand
            for n, lo, hi, y, opens, closes in sums:
                nc.tensor.matmul_mx(
                    out=y,
                    lhsT=w4_codes[:, b, 2 * n * P : 2 * (n + 1) * P].bitcast(FP4X4),
                    lhsT_scale=w4_plane[:, b, n * P : (n + 1) * P],
                    rhs=codes[:, lo - first : hi - first].bitcast(FP8X4),
                    rhs_scale=scales[:, lo - first : hi - first],
                    start=(b == 0 and opens),
                    stop=(b == PASSES - 1 and closes),
                )

        def square(y, name):
            squared = held(list(y.shape), F32, name)
            nc.scalar.activation(out=squared[:], in_=y, func=ACT.Square)
            return squared

        def finish(squared, dst, name):
            result = held(list(squared.shape), F32, name)
            nc.scalar.activation(out=result[:], in_=squared[:], func=ACT.Ln, bias=1.0)
            nc.sync.dma_start(out=dst, in_=result[:])

        def finish_early(n, squared):
            finish(squared, out[n * P : (n + 1) * P, :EARLY], "result_%d" % n)

        banks = [
            psum.tile([P, BANK], F32, name="y_%d" % n, tag=tag, bufs=bufs)
            for n, (tag, bufs) in enumerate((BANK_B, BANK_C, BANK_A))
        ]
        early_sums = [(n, lo, hi, banks[n][:, lo:hi], lo == 0, hi == EARLY) for n in range(N_TILES) for lo, hi in EARLY_RUNS]
        bank_late = psum.tile([P, N_TILES, LATE], F32, name="bank_late")
        late_sums = [(n, EARLY, M, bank_late[:, n, :], n == 0, n == N_TILES - 1) for n in range(N_TILES)]
        score(0, mx_d0, 0, early_sums)
        score(0, mx_d0, 0, late_sums)

        diff_late = held([P, PACK, LATE], F32, "diff_late")
        grouped_late = held([P, PACK * LATE], BF16, "grouped_late")

        def subtract_late(i, xa, xb):
            nc.vector.tensor_tensor(out=diff_late[:, i, :], in0=xa[:], in1=xb[:], op=ALU.subtract)

        def pick_late(i, tag_a, tag_b):
            xa = held_after(tag_a, [P, LATE], F32, "xa_late")
            return pick(h[PACK + i], EARLY, xa, held_after(tag_b, [P, LATE], F32, "xb_late"))

        picked = [pick_late(0, "page_%d" % SLICES, most_tags[1]), pick_late(1, xa_tag, "page_%d" % (SLICES + 1))]
        subtract_late(0, *picked[0])
        subtract_late(1, *picked[1])
        round_change(diff_late, grouped_late, 0, 2)
        score(1, quantise(grouped_d[1], "d_1_codes", "d_1"), 0, early_sums)
        last = held_after("grouped_d_1", [P, 2, 2, LATE], F32, "x_last")
        picked = [pick(h[PACK + 2 + u], EARLY, last[:, u, 0, :], last[:, u, 1, :]) for u in range(2)]
        subtract_late(2, *picked[0])
        subtract_late(3, *picked[1])

        finish_early(0, square(banks[0][:, :EARLY], "squared_0"))
        squared_1 = square(banks[1][:, :EARLY], "squared_1")
        round_change(diff_late, grouped_late, 2, PACK)
        score(1, quantise(grouped_late, "d_late_codes", "d_late"), EARLY, late_sums)
        finish_early(1, squared_1)
        finish_early(2, square(banks[2][:, :EARLY], "squared_2"))
        finish(square(bank_late[:], "squared_late"), out[:, EARLY:].rearrange("(n p) m -> p n m", p=P), "result_late")
